import numpy as np
import ml_dtypes


def mxq(x, axis, fmt="e4m3"):
    dtype, down = {"e4m3": (ml_dtypes.float8_e4m3fn, 7), "e5m2": (ml_dtypes.float8_e5m2, 14)}[fmt]
    v = np.moveaxis(np.asarray(x, np.float32).astype(ml_dtypes.bfloat16).astype(np.float64), axis, -1)
    blocks = v.reshape(v.shape[:-1] + (-1, 32))
    amax = np.abs(blocks).max(-1, keepdims=True)
    byte = np.maximum(np.where(amax > 0, np.frexp(amax)[1] - 1 + 127, 0) - down, 1)
    scale = np.exp2(byte - 127.0)
    codes = (blocks / scale).astype(np.float32).astype(dtype).astype(np.float64)
    return np.moveaxis((codes * scale).reshape(v.shape), -1, axis)


WIDE = False


def mx_kscale(k):
    if not WIDE:
        return np.ones(k)
    levels = np.array([10, -10, 5, -5, 0])
    if k % 512:
        return np.exp2(np.random.permutation(np.resize(levels, k // 32))).repeat(32)
    a = np.empty((k // 512, 16))
    for p in range(k // 512):
        a[p, :8] = np.random.permutation(np.resize(levels, 8))
        for g in range(8):
            far = levels[np.abs(levels - a[p, g]) >= 10]
            a[p, g + 8] = far[np.random.randint(len(far))]
    return np.exp2(a.ravel()).repeat(32)


BF16 = ml_dtypes.bfloat16


def bf(x):
    return np.asarray(x, np.float32).astype(BF16)


def f64(x):
    return np.asarray(x).astype(np.float64)


E2M1 = np.array([0.0, 0.5, 1.0, 1.5, 2.0, 3.0, 4.0, 6.0, -0.0, -0.5, -1.0, -1.5, -2.0, -3.0, -4.0, -6.0])


def pack_weight(w, fmt):
    k, n = w.shape
    w = f64(bf(w)).reshape(k // 32, 32, n)
    amax = np.abs(w).max(1)
    if fmt == "e4m3":
        byte = np.frexp(amax)[1] - 1 + 127 - 7
    else:
        mant, ex = np.frexp(amax / 6.0)
        byte = np.where(mant > 0.5, ex, ex - 1) + 127
    byte = np.clip(np.where(amax > 0, byte, 1), 1, 254)
    scaled = (w * np.exp2(127.0 - byte)[:, None, :]).reshape(k, n).astype(np.float32)
    by_word = np.ascontiguousarray(scaled.reshape(k // 512, 128, 4, n).transpose(0, 1, 3, 2))
    if fmt == "e4m3":
        words = by_word.astype(ml_dtypes.float8_e4m3fn).view(np.uint8)
    else:
        c = by_word.astype(ml_dtypes.float4_e2m1fn).view(np.uint8) & 0xF
        words = c[..., 0::2] | (c[..., 1::2] << 4)
    return np.ascontiguousarray(words), np.ascontiguousarray(byte.astype(np.uint8).reshape(k // 512, 16, n))


def unpack_weight(words, scales, fmt):
    g, p, n, _ = words.shape
    if fmt == "e4m3":
        vals = np.ascontiguousarray(words).view(ml_dtypes.float8_e4m3fn).astype(np.float64)
    else:
        nib = np.empty((g, p, n, 4), np.uint8)
        nib[..., 0::2] = words & 0xF
        nib[..., 1::2] = words >> 4
        vals = E2M1[nib]
    vals = vals * np.repeat(np.exp2(scales.astype(np.float64) - 127.0), 8, axis=1)[..., None]
    return vals.transpose(0, 1, 3, 2).reshape(g * 512, n)
def pack4(w):
    words, scales = pack_weight(w, "e2m1")
    return words.reshape(words.shape[0], 128, -1), scales


def unpack4(words, scales):
    return unpack_weight(words.reshape(words.shape[0], 128, -1, 2), scales, "e2m1")


BITS, D, Q, DOCS = 1024, 1536, 1024, 2048


def draw0():
    s, t = mx_kscale(D), mx_kscale(BITS)
    planes = 2.0 * np.random.standard_normal((BITS, D)) / np.sqrt(D) / s
    queries = np.random.standard_normal((Q, D)) * s
    offset = 0.5 * np.random.standard_normal(BITS)
    bit_gain = (1 + 0.1 * np.random.standard_normal(BITS)) * t
    codes = np.random.standard_normal((BITS, DOCS)) / np.sqrt(BITS) / t[:, None]
    codes_words, codes_scales = pack4(codes)
    return {"planes": bf(planes),
            "queries": bf(queries),
            "offset": bf(offset),
            "bit_gain": bf(bit_gain),
            "codes_words": codes_words,
            "codes_scales": codes_scales}


def core(planes, queries, offset, bit_gain, codes_words, codes_scales):
    h = mxq(f64(planes), 1, "e4m3") @ mxq(f64(queries), 1, "e4m3").T
    z = np.tanh(h + f64(offset)[:, None]) * f64(bit_gain)[:, None]
    return mxq(z, 0, "e4m3").T @ unpack4(codes_words, codes_scales)


def e4m3fn_bytes(y):
    return np.clip(np.asarray(y, np.float64), -448.0, 448.0).astype(np.float32).astype(ml_dtypes.float8_e4m3fn).view(np.uint8)


def e4m3fn_values(b):
    return np.asarray(b, np.uint8).view(ml_dtypes.float8_e4m3fn).astype(np.float64)


def setup_inputs():
    d = draw0()
    x0 = np.asarray(d['queries']).astype(np.float64)
    s = (np.max(np.abs(x0), axis=(0,), keepdims=True) / 448.0).astype(np.float32)
    out = {}
    for k, v in d.items():
        if k == 'queries':
            out['queries_bytes'] = e4m3fn_bytes(x0 / s.astype(np.float64))
            out['queries_scale'] = s
        else:
            out[k] = v
    return out


def reference(planes, queries_bytes, queries_scale, offset, bit_gain, codes_words, codes_scales):
    return core(planes, e4m3fn_values(queries_bytes) * queries_scale.astype(np.float64), offset, bit_gain, codes_words, codes_scales)

@@ -1,0 +1,296 @@
+from contextlib import ExitStack
+
+import concourse.mybir as mybir
+from concourse.masks import make_identity
+
+BITS, D, Q, DOCS = 1024, 1536, 1024, 2048
+FLOPS = 2 * BITS * D * Q + 2 * Q * BITS * DOCS
+
+F32 = mybir.dt.float32
+BF16 = mybir.dt.bfloat16
+I32 = mybir.dt.int32
+U32 = mybir.dt.uint32
+U8 = mybir.dt.uint8
+FP8 = mybir.dt.float8_e4m3fn
+FP8X4 = mybir.dt.float8_e4m3fn_x4
+FP4X4 = mybir.dt.float4_e2m1fn_x4
+ACT = mybir.ActivationFunctionType
+MULT = mybir.AluOpType.mult
+
+P = 128
+KD = D // 512
+KB = BITS // 512
+SLAB = 256
+NS = Q // SLAB
+NB = 512
+ND = DOCS // NB
+
+
+def tile_soft_hyperplane_hashing_s13_kernel(tc, planes, queries_bytes, queries_scale, offset, bit_gain, codes_words, codes_scales, out):
+    nc = tc.nc
+    with ExitStack() as ctx:
+        keep = ctx.enter_context(tc.tile_pool(name="keep", bufs=1))
+        work = ctx.enter_context(tc.tile_pool(name="work", bufs=3))
+        psum = ctx.enter_context(tc.psum_pool(name="psum", bufs=3))
+
+        ident = keep.tile([P, P], F32, name="ident")
+        ones = keep.tile([P, 1], F32, name="ones")
+        warm = keep.tile([P, 1], F32, name="warm")
+        q_scale = keep.tile([P, KD * 4], F32, name="q_scale")
+        off = keep.tile([P, KB * 4], BF16, name="off")
+        gain = keep.tile([P, KB * 4], BF16, name="gain")
+        q_bytes = [keep.tile([P, 2 * D], U8, name="q_bytes%d" % s) for s in range(NS)]
+        p_raw = [[keep.tile([P, 2, D], BF16, name="p_raw%d%d" % (g, h)) for h in range(2)] for g in range(KB)]
+        p_codes = [keep.tile([P, BITS], U32, name="p_codes%d" % g, align_bytes=64) for g in range(KD)]
+        p_scales = [keep.tile([P, BITS], U8, name="p_scales%d" % g, align_bytes=64) for g in range(KD)]
+        q_codes = [keep.tile([P, KD, SLAB], U32, name="q_codes%d" % s, align_bytes=64) for s in range(NS)]
+        q_scales = [keep.tile([P, KD, SLAB], U8, name="q_scales%d" % s, align_bytes=64) for s in range(NS)]
+        z_codes = [keep.tile([P, KB, SLAB], U32, name="z_codes%d" % s, align_bytes=64) for s in range(NS)]
+        z_scales = [keep.tile([P, KB, SLAB], U8, name="z_scales%d" % s, align_bytes=64) for s in range(NS)]
+        c_codes = keep.tile([P, KB, 2 * DOCS], U8, name="c_codes", align_bytes=64)
+        c_scales = keep.tile([P, KB, DOCS], U8, name="c_scales", align_bytes=64)
+
+        q_view = queries_bytes.rearrange("(s p i) k -> s p (i k)", p=P, i=2)
+        p_view = planes.rearrange("(g m t) k -> g m t k", m=P, t=4)
+        out_view = out.rearrange("(s p i) d -> s i p d", p=P, i=2)
+
+        def load_q(s):
+            nc.sync.dma_start(out=q_bytes[s][:], in_=q_view[s])
+
+        def load_p(g, h):
+            nc.sync.dma_start(out=p_raw[g][h][:], in_=p_view[g][:, 2 * h : 2 * h + 2, :])
+
+        q_cast = {}
+        banks = {}
+        p_group = {}
+        q_group = {}
+        tanh_out = {}
+        z_group = {}
+
+        def cast(s):
+            q_cast[s] = work.tile([P, 2, 2 * KD * P, 2], BF16, name="q_cast")
+            nc.vector.tensor_scalar(
+                out=q_cast[s][:].rearrange("p u w e -> p w u e"),
+                in0=q_bytes[s][:].bitcast(FP8).rearrange("p (w u e) -> p w u e", u=2, e=2),
+                scalar1=ones[:, 0:1],
+                scalar2=None,
+                op0=MULT,
+            )
+
+        def q_transpose(s):
+            words = q_cast[s][:].rearrange("p u w e -> p (u w e)").bitcast(F32)
+            for g in range(KD):
+                bank = psum.tile([P, 512], F32, name="tbank")
+                for u in range(2):
+                    for i in range(2):
+                        w0 = u * 2 * KD * P + i * KD * P + g * P
+                        nc.tensor.transpose(bank[:, u * 256 + i * P : u * 256 + (i + 1) * P], words[:, w0 : w0 + P], ident[:])
+                banks["q", s, g] = bank
+
+        def q_exit(s, g):
+            grouped = work.tile([P, SLAB, 2, 2], BF16, name="q_group", align_bytes=64)
+            bank = banks["q", s, g]
+            nc.vector.tensor_tensor(
+                out=grouped[:],
+                in0=bank[:].bitcast(BF16).rearrange("p (u c e) -> p c u e", u=2, e=2),
+                in1=q_scale[:, 4 * g : 4 * g + 4].rearrange("p (o u e) -> p o u e", o=1, u=2).to_broadcast([P, SLAB, 2, 2]),
+                op=MULT,
+            )
+            q_group[s, g] = grouped
+
+        def q_quant(s, g):
+            nc.vector.quantize_mx(
+                out=q_codes[s][:, g, :].bitcast(FP8X4),
+                scales=q_scales[s][:, g, :],
+                in_=q_group[s, g][:].rearrange("p c u e -> p (c u e)"),
+            )
+
+        def p_transpose(gb, h):
+            for g in range(KD):
+                bank = psum.tile([P, 512], F32, name="obank")
+                for u in range(2):
+                    for i in range(2):
+                        words = p_raw[gb][h][:, i, :].bitcast(F32)
+                        nc.tensor.transpose(
+                            bank[:, u * 256 + i * P : u * 256 + (i + 1) * P],
+                            words[:, 256 * g + u : 256 * (g + 1) : 2],
+                            ident[:],
+                        )
+                banks["p", gb, h, g] = bank
+
+        def p_exit(gb, h, g, eng):
+            grouped = work.tile([P, 256, 4], BF16, name="p_group", align_bytes=64, bufs=4)
+            dst = grouped[:].rearrange("p c t -> p (c t)").bitcast(F32).rearrange("p (c u) -> p c u", u=2)
+            bank_view = banks["p", gb, h, g][:].rearrange("p (u c) -> p c u", u=2)
+            if eng == "s":
+                nc.scalar.copy(out=dst, in_=bank_view)
+            else:
+                nc.vector.tensor_copy(out=dst, in_=bank_view)
+            p_group[gb, h, g] = grouped
+
+        def p_quant(gb, h, g):
+            cols = slice(gb * 512 + h * 256, gb * 512 + h * 256 + 256)
+            nc.vector.quantize_mx(
+                out=p_codes[g][:, cols].bitcast(FP8X4),
+                scales=p_scales[g][:, cols],
+                in_=p_group[gb, h, g][:].rearrange("p c t -> p (c t)"),
+            )
+
+        def project(s, gb):
+            th = work.tile([P, 4, SLAB], F32, name="th")
+            for tp in range(2):
+                bank = psum.tile([P, 2, SLAB], F32, name="hbank", bufs=2)
+                for t2 in range(2):
+                    c0 = gb * 512 + (tp * 2 + t2) * P
+                    for g in range(KD):
+                        nc.tensor.matmul_mx(
+                            out=bank[:, t2, :],
+                            lhsT=p_codes[g][:, c0 : c0 + P].bitcast(FP8X4),
+                            lhsT_scale=p_scales[g][:, c0 : c0 + P],
+                            rhs=q_codes[s][:, g, :].bitcast(FP8X4),
+                            rhs_scale=q_scales[s][:, g, :],
+                            start=(g == 0),
+                            stop=(g == KD - 1),
+                        )
+                for t2 in range(2):
+                    t = tp * 2 + t2
+                    nc.scalar.activation(out=th[:, t, :], in_=bank[:, t2, :], func=ACT.Tanh, bias=off[:, gb * 4 + t : gb * 4 + t + 1])
+            tanh_out[s, gb] = th
+
+        def weight(s, gb):
+            zg = work.tile([P, SLAB, 4], BF16, name="z_group", align_bytes=64)
+            nc.vector.tensor_tensor(
+                out=zg[:],
+                in0=tanh_out[s, gb][:].rearrange("p t n -> p n t"),
+                in1=gain[:, gb * 4 : gb * 4 + 4].rearrange("p (o t) -> p o t", o=1).to_broadcast([P, SLAB, 4]),
+                op=MULT,
+            )
+            z_group[s, gb] = zg
+
+        def z_quant(s, gb):
+            nc.vector.quantize_mx(
+                out=z_codes[s][:, gb, :].bitcast(FP8X4),
+                scales=z_scales[s][:, gb, :],
+                in_=z_group[s, gb][:].rearrange("p n t -> p (n t)"),
+            )
+
+        def score(s, i, engines):
+            for half in range(2):
+                ot = work.tile([P, 2, NB], F32, name="ot", bufs=6)
+                for b in range(2):
+                    d = half * 2 + b
+                    bank = psum.tile([P, NB], F32, name="obank")
+                    for gb in range(KB):
+                        nc.tensor.matmul_mx(
+                            out=bank[:],
+                            lhsT=z_codes[s][:, gb, i * P : (i + 1) * P].bitcast(FP8X4),
+                            lhsT_scale=z_scales[s][:, gb, i * P : (i + 1) * P],
+                            rhs=c_codes[:, gb, d * 2 * NB : (d + 1) * 2 * NB].bitcast(FP4X4),
+                            rhs_scale=c_scales[:, gb, d * NB : (d + 1) * NB],
+                            start=(gb == 0),
+                            stop=(gb == KB - 1),
+                        )
+                    if engines[d] == "s":
+                        nc.scalar.copy(out=ot[:, b, :], in_=bank[:])
+                    else:
+                        nc.vector.tensor_copy(out=ot[:, b, :], in_=bank[:])
+                nc.sync.dma_start(out=out_view[s, i][:, half * 1024 : (half + 1) * 1024], in_=ot[:].rearrange("p b n -> p (b n)"))
+
+        with tc.manual_schedule():
+            load_q(0)
+            nc.scalar.dma_start(out=q_scale[:].rearrange("p (g t) -> p g t", t=4), in_=queries_scale.rearrange("o (g p t) -> p (o g) t", p=P, t=4))
+            nc.scalar.dma_start(out=off[:].rearrange("p (g t) -> p g t", t=4), in_=offset.rearrange("(g p t) -> p g t", p=P, t=4))
+            nc.scalar.dma_start(out=gain[:].rearrange("p (g t) -> p g t", t=4), in_=bit_gain.rearrange("(g p t) -> p g t", p=P, t=4))
+            nc.vector.memset(ones[:], 1.0)
+            nc.scalar.activation(out=warm[:], in_=ones[:], func=ACT.Tanh)
+            make_identity(nc, ident[:])
+            nc.gpsimd.memset(c_scales[:].rearrange("p g n -> p (g n)").bitcast(U32), 0)
+            load_p(0, 0)
+            load_p(0, 1)
+            load_p(1, 0)
+            load_p(1, 1)
+            load_q(1)
+            load_q(2)
+            nc.sync.dma_start(out=c_codes[:].rearrange("p g n -> p g n").bitcast(I32), in_=codes_words.rearrange("g p n -> p g n").bitcast(I32))
+            for qd in range(4):
+                nc.sync.dma_start(
+                    out=c_scales[32 * qd : 32 * qd + 4, :, :].bitcast(I32),
+                    in_=codes_scales.rearrange("g q n -> q g n")[4 * qd : 4 * qd + 4].bitcast(I32),
+                )
+            load_q(3)
+
+            def exits(gb, h, engs="sss"):
+                for g in range(KD):
+                    p_exit(gb, h, g, engs[g])
+
+            def quants(gb, h):
+                for g in range(KD):
+                    p_quant(gb, h, g)
+
+            def xq(s, a):
+                for g in a:
+                    q_exit(s, g)
+                    if g > 0:
+                        q_quant(s, g - 1)
+            cast(0)
+            q_transpose(0)
+            p_transpose(0, 0)
+            exits(0, 0)
+            xq(0, (0, 1))
+            q_exit(0, 2)
+            q_quant(0, 1)
+            quants(0, 0)
+            q_quant(0, 2)
+            p_transpose(0, 1)
+            exits(0, 1)
+            quants(0, 1)
+            p_transpose(1, 0)
+            exits(1, 0)
+            cast(1)
+            project(0, 0)
+            q_transpose(1)
+            quants(1, 0)
+            q_exit(1, 0)
+            p_transpose(1, 1)
+            exits(1, 1)
+            weight(0, 0)
+            q_exit(1, 1)
+            q_quant(1, 0)
+            quants(1, 1)
+            project(0, 1)
+            q_exit(1, 2)
+            q_quant(1, 1)
+            z_quant(0, 0)
+            q_quant(1, 2)
+            project(1, 0)
+            cast(2)
+            weight(0, 1)
+            q_transpose(2)
+            project(1, 1)
+            q_exit(2, 0)
+            z_quant(0, 1)
+            for s in range(1, NS):
+                if s + 1 < NS:
+                    q_exit(s + 1, 1)
+                    q_quant(s + 1, 0)
+                weight(s, 0)
+                if s + 1 < NS:
+                    q_exit(s + 1, 2)
+                    q_quant(s + 1, 1)
+                score(s - 1, 0, "ssss")
+                z_quant(s, 0)
+                weight(s, 1)
+                if s + 1 < NS:
+                    q_quant(s + 1, 2)
+                    project(s + 1, 0)
+                if s + 2 < NS:
+                    cast(s + 2)
+                    q_transpose(s + 2)
+                z_quant(s, 1)
+                if s + 2 < NS:
+                    q_exit(s + 2, 0)
+                score(s - 1, 1, "ssss" if s < 3 else "svsv")
+                if s + 1 < NS:
+                    project(s + 1, 1)
+            score(3, 0, "svsv")
+            score(3, 1, "svsv")

@@ -34,6 +34,7 @@ def tile_soft_hyperplane_hashing_s13_kernel(tc, planes, queries_bytes, queries_s
         psum = ctx.enter_context(tc.psum_pool(name="psum", bufs=3))
 
         ident = keep.tile([P, P], F32, name="ident")
+        zeros = keep.tile([P, 512], BF16, name="zeros")
         ones = keep.tile([P, 1], F32, name="ones")
         warm = keep.tile([P, 1], F32, name="warm")
         q_scale = keep.tile([P, KD * 4], F32, name="q_scale")
@@ -66,6 +67,11 @@ def tile_soft_hyperplane_hashing_s13_kernel(tc, planes, queries_bytes, queries_s
         q_group = {}
         tanh_out = {}
         z_group = {}
+
+        def dummy(n):
+            bank = psum.tile([P, 512], F32, name="hbank", bufs=2)
+            for j in range(n):
+                nc.tensor.matmul(bank[:], lhsT=zeros[:, 0:P], rhs=zeros[:], start=True, stop=True)
 
         def cast(s):
             q_cast[s] = work.tile([P, 2, 2 * KD * P, 2], BF16, name="q_cast")
@@ -105,8 +111,10 @@ def tile_soft_hyperplane_hashing_s13_kernel(tc, planes, queries_bytes, queries_s
                 in_=q_group[s, g][:].rearrange("p c u e -> p (c u e)"),
             )
 
-        def p_transpose(gb, h):
+        def p_transpose(gb, h, dum=()):
             for g in range(KD):
+                if g in dum:
+                    dummy(2)
                 bank = psum.tile([P, 512], F32, name="obank")
                 for u in range(2):
                     for i in range(2):
@@ -160,9 +168,9 @@ def tile_soft_hyperplane_hashing_s13_kernel(tc, planes, queries_bytes, queries_s
         def weight(s, gb):
             zg = work.tile([P, SLAB, 4], BF16, name="z_group", align_bytes=64)
             nc.vector.tensor_tensor(
-                out=zg[:],
-                in0=tanh_out[s, gb][:].rearrange("p t n -> p n t"),
-                in1=gain[:, gb * 4 : gb * 4 + 4].rearrange("p (o t) -> p o t", o=1).to_broadcast([P, SLAB, 4]),
+                out=zg[:].rearrange("p (c i) t -> p c t i", i=4),
+                in0=tanh_out[s, gb][:].rearrange("p t (c i) -> p c t i", i=4),
+                in1=gain[:, gb * 4 : gb * 4 + 4].rearrange("p (o t i) -> p o t i", o=1, i=1).to_broadcast([P, SLAB // 4, 4, 4]),
                 op=MULT,
             )
             z_group[s, gb] = zg
@@ -201,6 +209,8 @@ def tile_soft_hyperplane_hashing_s13_kernel(tc, planes, queries_bytes, queries_s
             nc.scalar.dma_start(out=q_scale[:].rearrange("p (g t) -> p g t", t=4), in_=queries_scale.rearrange("o (g p t) -> p (o g) t", p=P, t=4))
             nc.scalar.dma_start(out=off[:].rearrange("p (g t) -> p g t", t=4), in_=offset.rearrange("(g p t) -> p g t", p=P, t=4))
             nc.scalar.dma_start(out=gain[:].rearrange("p (g t) -> p g t", t=4), in_=bit_gain.rearrange("(g p t) -> p g t", p=P, t=4))
+            nc.vector.memset(zeros[:], 0.0)
+            dummy(8)
             nc.vector.memset(ones[:], 1.0)
             nc.scalar.activation(out=warm[:], in_=ones[:], func=ACT.Tanh)
             make_identity(nc, ident[:])
@@ -234,17 +244,17 @@ def tile_soft_hyperplane_hashing_s13_kernel(tc, planes, queries_bytes, queries_s
                         q_quant(s, g - 1)
             cast(0)
             q_transpose(0)
-            p_transpose(0, 0)
+            p_transpose(0, 0, (0, 2))
             exits(0, 0)
             xq(0, (0, 1))
             q_exit(0, 2)
             q_quant(0, 1)
             quants(0, 0)
             q_quant(0, 2)
-            p_transpose(0, 1)
+            p_transpose(0, 1, (1,))
             exits(0, 1)
             quants(0, 1)
-            p_transpose(1, 0)
+            p_transpose(1, 0, (0, 2))
             exits(1, 0)
             cast(1)
             project(0, 0)

@@ -55,8 +55,10 @@ def tile_soft_hyperplane_hashing_s13_kernel(tc, planes, queries_bytes, queries_s
         p_view = planes.rearrange("(g m t) k -> g m t k", m=P, t=4)
         out_view = out.rearrange("(s p i) d -> s i p d", p=P, i=2)
 
-        def load_q(s):
-            nc.sync.dma_start(out=q_bytes[s][:], in_=q_view[s])
+        def load_q(s, parts=1):
+            w = 2 * D // parts
+            for i in range(parts):
+                nc.sync.dma_start(out=q_bytes[s][:, i * w : (i + 1) * w], in_=q_view[s][:, i * w : (i + 1) * w])
 
         def load_p(g, h):
             nc.sync.dma_start(out=p_raw[g][h][:], in_=p_view[g][:, 2 * h : 2 * h + 2, :])
@@ -73,15 +75,17 @@ def tile_soft_hyperplane_hashing_s13_kernel(tc, planes, queries_bytes, queries_s
             for j in range(n):
                 nc.tensor.matmul(bank[:], lhsT=zeros[:, 0:P], rhs=zeros[:], start=True, stop=True)
 
-        def cast(s):
+        def cast(s, parts=1):
             q_cast[s] = work.tile([P, 2, 2 * KD * P, 2], BF16, name="q_cast")
-            nc.vector.tensor_scalar(
-                out=q_cast[s][:].rearrange("p u w e -> p w u e"),
-                in0=q_bytes[s][:].bitcast(FP8).rearrange("p (w u e) -> p w u e", u=2, e=2),
-                scalar1=ones[:, 0:1],
-                scalar2=None,
-                op0=MULT,
-            )
+            w = 2 * KD * P // parts
+            for i in range(parts):
+                nc.vector.tensor_scalar(
+                    out=q_cast[s][:, :, i * w : (i + 1) * w, :].rearrange("p u w e -> p w u e"),
+                    in0=q_bytes[s][:, 4 * i * w : 4 * (i + 1) * w].bitcast(FP8).rearrange("p (w u e) -> p w u e", u=2, e=2),
+                    scalar1=ones[:, 0:1],
+                    scalar2=None,
+                    op0=MULT,
+                )
 
         def q_transpose(s):
             words = q_cast[s][:].rearrange("p u w e -> p (u w e)").bitcast(F32)
@@ -127,7 +131,7 @@ def tile_soft_hyperplane_hashing_s13_kernel(tc, planes, queries_bytes, queries_s
                 banks["p", gb, h, g] = bank
 
         def p_exit(gb, h, g, eng):
-            grouped = work.tile([P, 256, 4], BF16, name="p_group", align_bytes=64, bufs=4)
+            grouped = work.tile([P, 256, 4], BF16, name="p_group", align_bytes=64, bufs=8)
             dst = grouped[:].rearrange("p c t -> p (c t)").bitcast(F32).rearrange("p (c u) -> p c u", u=2)
             bank_view = banks["p", gb, h, g][:].rearrange("p (u c) -> p c u", u=2)
             if eng == "s":
@@ -167,12 +171,13 @@ def tile_soft_hyperplane_hashing_s13_kernel(tc, planes, queries_bytes, queries_s
 
         def weight(s, gb):
             zg = work.tile([P, SLAB, 4], BF16, name="z_group", align_bytes=64)
-            nc.vector.tensor_tensor(
-                out=zg[:].rearrange("p (c i) t -> p c t i", i=4),
-                in0=tanh_out[s, gb][:].rearrange("p t (c i) -> p c t i", i=4),
-                in1=gain[:, gb * 4 : gb * 4 + 4].rearrange("p (o t i) -> p o t i", o=1, i=1).to_broadcast([P, SLAB // 4, 4, 4]),
-                op=MULT,
-            )
+            for i in range(2):
+                nc.gpsimd.tensor_tensor(
+                    out=zg[:, i * P : (i + 1) * P, :],
+                    in0=tanh_out[s, gb][:, :, i * P : (i + 1) * P].rearrange("p t n -> p n t"),
+                    in1=gain[:, gb * 4 : gb * 4 + 4].rearrange("p (o t) -> p o t", o=1).to_broadcast([P, P, 4]),
+                    op=MULT,
+                )
             z_group[s, gb] = zg
 
         def z_quant(s, gb):
@@ -184,7 +189,7 @@ def tile_soft_hyperplane_hashing_s13_kernel(tc, planes, queries_bytes, queries_s
 
         def score(s, i, engines):
             for half in range(2):
-                ot = work.tile([P, 2, NB], F32, name="ot", bufs=6)
+                ot = work.tile([P, 2, NB], F32, name="ot", bufs=8)
                 for b in range(2):
                     d = half * 2 + b
                     bank = psum.tile([P, NB], F32, name="obank")
@@ -202,10 +207,13 @@ def tile_soft_hyperplane_hashing_s13_kernel(tc, planes, queries_bytes, queries_s
                         nc.scalar.copy(out=ot[:, b, :], in_=bank[:])
                     else:
                         nc.vector.tensor_copy(out=ot[:, b, :], in_=bank[:])
-                nc.sync.dma_start(out=out_view[s, i][:, half * 1024 : (half + 1) * 1024], in_=ot[:].rearrange("p b n -> p (b n)"))
+                    if s == NS - 1 and i == 1:
+                        nc.sync.dma_start(out=out_view[s, i][:, d * NB : (d + 1) * NB], in_=ot[:, b, :])
+                if not (s == NS - 1 and i == 1):
+                    nc.sync.dma_start(out=out_view[s, i][:, half * 1024 : (half + 1) * 1024], in_=ot[:].rearrange("p b n -> p (b n)"))
 
         with tc.manual_schedule():
-            load_q(0)
+            load_q(0, 2)
             nc.scalar.dma_start(out=q_scale[:].rearrange("p (g t) -> p g t", t=4), in_=queries_scale.rearrange("o (g p t) -> p (o g) t", p=P, t=4))
             nc.scalar.dma_start(out=off[:].rearrange("p (g t) -> p g t", t=4), in_=offset.rearrange("(g p t) -> p g t", p=P, t=4))
             nc.scalar.dma_start(out=gain[:].rearrange("p (g t) -> p g t", t=4), in_=bit_gain.rearrange("(g p t) -> p g t", p=P, t=4))
@@ -242,7 +250,7 @@ def tile_soft_hyperplane_hashing_s13_kernel(tc, planes, queries_bytes, queries_s
                     q_exit(s, g)
                     if g > 0:
                         q_quant(s, g - 1)
-            cast(0)
+            cast(0, 2)
             q_transpose(0)
             p_transpose(0, 0, (0, 2))
             exits(0, 0)

@@ -171,13 +171,12 @@ def tile_soft_hyperplane_hashing_s13_kernel(tc, planes, queries_bytes, queries_s
 
         def weight(s, gb):
             zg = work.tile([P, SLAB, 4], BF16, name="z_group", align_bytes=64)
-            for i in range(2):
-                nc.gpsimd.tensor_tensor(
-                    out=zg[:, i * P : (i + 1) * P, :],
-                    in0=tanh_out[s, gb][:, :, i * P : (i + 1) * P].rearrange("p t n -> p n t"),
-                    in1=gain[:, gb * 4 : gb * 4 + 4].rearrange("p (o t) -> p o t", o=1).to_broadcast([P, P, 4]),
-                    op=MULT,
-                )
+            nc.vector.tensor_tensor(
+                out=zg[:].rearrange("p (c i) t -> p c t i", i=4),
+                in0=tanh_out[s, gb][:].rearrange("p t (c i) -> p c t i", i=4),
+                in1=gain[:, gb * 4 : gb * 4 + 4].rearrange("p (o t i) -> p o t i", o=1, i=1).to_broadcast([P, SLAB // 4, 4, 4]),
+                op=MULT,
+            )
             z_group[s, gb] = zg
 
         def z_quant(s, gb):
@@ -252,63 +251,77 @@ def tile_soft_hyperplane_hashing_s13_kernel(tc, planes, queries_bytes, queries_s
                         q_quant(s, g - 1)
             cast(0, 2)
             q_transpose(0)
-            p_transpose(0, 0, (0, 2))
+            p_transpose(0, 0)
             exits(0, 0)
-            xq(0, (0, 1))
+            q_exit(0, 0)
+            q_exit(0, 1)
+            q_quant(0, 0)
             q_exit(0, 2)
             q_quant(0, 1)
             quants(0, 0)
             q_quant(0, 2)
-            p_transpose(0, 1, (1,))
+            p_transpose(0, 1, (0,))
             exits(0, 1)
             quants(0, 1)
-            p_transpose(1, 0, (0, 2))
+            p_transpose(1, 0, (0,))
             exits(1, 0)
             cast(1)
-            project(0, 0)
-            q_transpose(1)
+            cast(2)
             quants(1, 0)
-            q_exit(1, 0)
-            p_transpose(1, 1)
+            p_transpose(1, 1, (0,))
             exits(1, 1)
-            weight(0, 0)
-            q_exit(1, 1)
-            q_quant(1, 0)
+            q_transpose(1)
+            project(0, 0)
+            q_exit(1, 0)
             quants(1, 1)
             project(0, 1)
+            q_exit(1, 1)
+            q_quant(1, 0)
             q_exit(1, 2)
             q_quant(1, 1)
-            z_quant(0, 0)
+            weight(0, 0)
             q_quant(1, 2)
-            project(1, 0)
-            cast(2)
-            weight(0, 1)
             q_transpose(2)
-            project(1, 1)
+            weight(0, 1)
+            z_quant(0, 0)
+            project(1, 0)
             q_exit(2, 0)
             z_quant(0, 1)
-            for s in range(1, NS):
-                if s + 1 < NS:
-                    q_exit(s + 1, 1)
-                    q_quant(s + 1, 0)
-                weight(s, 0)
-                if s + 1 < NS:
-                    q_exit(s + 1, 2)
-                    q_quant(s + 1, 1)
-                score(s - 1, 0, "ssss")
-                z_quant(s, 0)
-                weight(s, 1)
-                if s + 1 < NS:
-                    q_quant(s + 1, 2)
-                    project(s + 1, 0)
-                if s + 2 < NS:
-                    cast(s + 2)
-                    q_transpose(s + 2)
-                z_quant(s, 1)
-                if s + 2 < NS:
-                    q_exit(s + 2, 0)
-                score(s - 1, 1, "ssss" if s < 3 else "svsv")
-                if s + 1 < NS:
-                    project(s + 1, 1)
+            project(1, 1)
+            q_exit(2, 1)
+            q_quant(2, 0)
+            cast(3)
+            score(0, 0, "ssss")
+            q_exit(2, 2)
+            q_quant(2, 1)
+            weight(1, 0)
+            q_quant(2, 2)
+            weight(1, 1)
+            z_quant(1, 0)
+            score(0, 1, "ssss")
+            q_transpose(3)
+            project(2, 0)
+            q_exit(3, 0)
+            z_quant(1, 1)
+            project(2, 1)
+            q_exit(3, 1)
+            q_quant(3, 0)
+            q_exit(3, 2)
+            q_quant(3, 1)
+            score(1, 0, "ssss")
+            weight(2, 0)
+            q_quant(3, 2)
+            weight(2, 1)
+            z_quant(2, 0)
+            score(1, 1, "ssss")
+            project(3, 0)
+            z_quant(2, 1)
+            project(3, 1)
+            weight(3, 0)
+            score(2, 0, "ssss")
+            weight(3, 1)
+            z_quant(3, 0)
+            z_quant(3, 1)
+            score(2, 1, "ssvs")
             score(3, 0, "svsv")
             score(3, 1, "svsv")

@@ -214,19 +214,19 @@ def tile_soft_hyperplane_hashing_s13_kernel(tc, planes, queries_bytes, queries_s
         with tc.manual_schedule():
             load_q(0, 2)
             nc.scalar.dma_start(out=q_scale[:].rearrange("p (g t) -> p g t", t=4), in_=queries_scale.rearrange("o (g p t) -> p (o g) t", p=P, t=4))
-            nc.scalar.dma_start(out=off[:].rearrange("p (g t) -> p g t", t=4), in_=offset.rearrange("(g p t) -> p g t", p=P, t=4))
-            nc.scalar.dma_start(out=gain[:].rearrange("p (g t) -> p g t", t=4), in_=bit_gain.rearrange("(g p t) -> p g t", p=P, t=4))
             nc.vector.memset(zeros[:], 0.0)
             dummy(8)
             nc.vector.memset(ones[:], 1.0)
             nc.scalar.activation(out=warm[:], in_=ones[:], func=ACT.Tanh)
             make_identity(nc, ident[:])
             nc.gpsimd.memset(c_scales[:].rearrange("p g n -> p (g n)").bitcast(U32), 0)
+            load_q(1)
             load_p(0, 0)
             load_p(0, 1)
             load_p(1, 0)
             load_p(1, 1)
-            load_q(1)
+            nc.sync.dma_start(out=off[:].rearrange("p (g t) -> p g t", t=4), in_=offset.rearrange("(g p t) -> p g t", p=P, t=4))
+            nc.sync.dma_start(out=gain[:].rearrange("p (g t) -> p g t", t=4), in_=bit_gain.rearrange("(g p t) -> p g t", p=P, t=4))
             load_q(2)
             nc.sync.dma_start(out=c_codes[:].rearrange("p g n -> p g n").bitcast(I32), in_=codes_words.rearrange("g p n -> p g n").bitcast(I32))
             for qd in range(4):
@@ -249,8 +249,9 @@ def tile_soft_hyperplane_hashing_s13_kernel(tc, planes, queries_bytes, queries_s
                     q_exit(s, g)
                     if g > 0:
                         q_quant(s, g - 1)
-            cast(0, 2)
+            cast(0, parts=2)
             q_transpose(0)
+            cast(1)
             p_transpose(0, 0)
             exits(0, 0)
             q_exit(0, 0)
@@ -263,14 +264,12 @@ def tile_soft_hyperplane_hashing_s13_kernel(tc, planes, queries_bytes, queries_s
             p_transpose(0, 1, (0,))
             exits(0, 1)
             quants(0, 1)
-            p_transpose(1, 0, (0,))
+            q_transpose(1)
+            p_transpose(1, 0)
             exits(1, 0)
-            cast(1)
-            cast(2)
             quants(1, 0)
             p_transpose(1, 1, (0,))
             exits(1, 1)
-            q_transpose(1)
             project(0, 0)
             q_exit(1, 0)
             quants(1, 1)
@@ -279,38 +278,39 @@ def tile_soft_hyperplane_hashing_s13_kernel(tc, planes, queries_bytes, queries_s
             q_quant(1, 0)
             q_exit(1, 2)
             q_quant(1, 1)
-            weight(0, 0)
             q_quant(1, 2)
+            project(1, 0)
+            cast(2)
+            weight(0, 0)
+            project(1, 1)
             q_transpose(2)
             weight(0, 1)
             z_quant(0, 0)
-            project(1, 0)
-            q_exit(2, 0)
             z_quant(0, 1)
-            project(1, 1)
+            q_exit(2, 0)
             q_exit(2, 1)
             q_quant(2, 0)
             cast(3)
             score(0, 0, "ssss")
             q_exit(2, 2)
             q_quant(2, 1)
-            weight(1, 0)
             q_quant(2, 2)
+            weight(1, 0)
             weight(1, 1)
             z_quant(1, 0)
             score(0, 1, "ssss")
             q_transpose(3)
             project(2, 0)
-            q_exit(3, 0)
             z_quant(1, 1)
+            q_exit(3, 0)
             project(2, 1)
             q_exit(3, 1)
             q_quant(3, 0)
             q_exit(3, 2)
             q_quant(3, 1)
             score(1, 0, "ssss")
-            weight(2, 0)
             q_quant(3, 2)
+            weight(2, 0)
             weight(2, 1)
             z_quant(2, 0)
             score(1, 1, "ssss")

from contextlib import ExitStack

import concourse.mybir as mybir
from concourse.masks import make_identity

BITS, D, Q, DOCS = 1024, 1536, 1024, 2048
FLOPS = 2 * BITS * D * Q + 2 * Q * BITS * DOCS

F32 = mybir.dt.float32
BF16 = mybir.dt.bfloat16
I32 = mybir.dt.int32
U32 = mybir.dt.uint32
U8 = mybir.dt.uint8
FP8 = mybir.dt.float8_e4m3fn
FP8X4 = mybir.dt.float8_e4m3fn_x4
FP4X4 = mybir.dt.float4_e2m1fn_x4
ACT = mybir.ActivationFunctionType
MULT = mybir.AluOpType.mult

P = 128
KD = D // 512
KB = BITS // 512
SLAB = 256
NS = Q // SLAB
NB = 512
ND = DOCS // NB


def tile_soft_hyperplane_hashing_s13_kernel(tc, planes, queries_bytes, queries_scale, offset, bit_gain, codes_words, codes_scales, out):
    nc = tc.nc
    with ExitStack() as ctx:
        keep = ctx.enter_context(tc.tile_pool(name="keep", bufs=1))
        work = ctx.enter_context(tc.tile_pool(name="work", bufs=3))
        psum = ctx.enter_context(tc.psum_pool(name="psum", bufs=3))

        ident = keep.tile([P, P], F32, name="ident")
        zeros = keep.tile([P, 512], BF16, name="zeros")
        ones = keep.tile([P, 1], F32, name="ones")
        warm = keep.tile([P, 1], F32, name="warm")
        q_scale = keep.tile([P, KD * 4], F32, name="q_scale")
        off = keep.tile([P, KB * 4], BF16, name="off")
        gain = keep.tile([P, KB * 4], BF16, name="gain")
        q_bytes = [keep.tile([P, 2 * D], U8, name="q_bytes%d" % s) for s in range(NS)]
        p_raw = [[keep.tile([P, 2, D], BF16, name="p_raw%d%d" % (g, h)) for h in range(2)] for g in range(KB)]
        p_codes = [keep.tile([P, BITS], U32, name="p_codes%d" % g, align_bytes=64) for g in range(KD)]
        p_scales = [keep.tile([P, BITS], U8, name="p_scales%d" % g, align_bytes=64) for g in range(KD)]
        q_codes = [keep.tile([P, KD, SLAB], U32, name="q_codes%d" % s, align_bytes=64) for s in range(NS)]
        q_scales = [keep.tile([P, KD, SLAB], U8, name="q_scales%d" % s, align_bytes=64) for s in range(NS)]
        z_codes = [keep.tile([P, KB, SLAB], U32, name="z_codes%d" % s, align_bytes=64) for s in range(NS)]
        z_scales = [keep.tile([P, KB, SLAB], U8, name="z_scales%d" % s, align_bytes=64) for s in range(NS)]
        c_codes = keep.tile([P, KB, 2 * DOCS], U8, name="c_codes", align_bytes=64)
        c_scales = keep.tile([P, KB, DOCS], U8, name="c_scales", align_bytes=64)

        q_view = queries_bytes.rearrange("(s p i) k -> s p (i k)", p=P, i=2)
        p_view = planes.rearrange("(g m t) k -> g m t k", m=P, t=4)
        out_view = out.rearrange("(s p i) d -> s i p d", p=P, i=2)

        def load_q(s, parts=1):
            w = 2 * D // parts
            for i in range(parts):
                nc.sync.dma_start(out=q_bytes[s][:, i * w : (i + 1) * w], in_=q_view[s][:, i * w : (i + 1) * w])

        def load_p(g, h):
            nc.sync.dma_start(out=p_raw[g][h][:], in_=p_view[g][:, 2 * h : 2 * h + 2, :])

        q_cast = {}
        banks = {}
        p_group = {}
        q_group = {}
        tanh_out = {}
        z_group = {}

        def dummy(n):
            bank = psum.tile([P, 512], F32, name="hbank", bufs=2)
            for j in range(n):
                nc.tensor.matmul(bank[:], lhsT=zeros[:, 0:P], rhs=zeros[:], start=True, stop=True)

        def cast(s, parts=1):
            q_cast[s] = work.tile([P, 2, 2 * KD * P, 2], BF16, name="q_cast")
            w = 2 * KD * P // parts
            for i in range(parts):
                nc.vector.tensor_scalar(
                    out=q_cast[s][:, :, i * w : (i + 1) * w, :].rearrange("p u w e -> p w u e"),
                    in0=q_bytes[s][:, 4 * i * w : 4 * (i + 1) * w].bitcast(FP8).rearrange("p (w u e) -> p w u e", u=2, e=2),
                    scalar1=ones[:, 0:1],
                    scalar2=None,
                    op0=MULT,
                )

        def q_transpose(s):
            words = q_cast[s][:].rearrange("p u w e -> p (u w e)").bitcast(F32)
            for g in range(KD):
                bank = psum.tile([P, 512], F32, name="tbank")
                for u in range(2):
                    for i in range(2):
                        w0 = u * 2 * KD * P + i * KD * P + g * P
                        nc.tensor.transpose(bank[:, u * 256 + i * P : u * 256 + (i + 1) * P], words[:, w0 : w0 + P], ident[:])
                banks["q", s, g] = bank

        def q_exit(s, g):
            grouped = work.tile([P, SLAB, 2, 2], BF16, name="q_group", align_bytes=64)
            bank = banks["q", s, g]
            nc.vector.tensor_tensor(
                out=grouped[:],
                in0=bank[:].bitcast(BF16).rearrange("p (u c e) -> p c u e", u=2, e=2),
                in1=q_scale[:, 4 * g : 4 * g + 4].rearrange("p (o u e) -> p o u e", o=1, u=2).to_broadcast([P, SLAB, 2, 2]),
                op=MULT,
            )
            q_group[s, g] = grouped

        def q_quant(s, g):
            nc.vector.quantize_mx(
                out=q_codes[s][:, g, :].bitcast(FP8X4),
                scales=q_scales[s][:, g, :],
                in_=q_group[s, g][:].rearrange("p c u e -> p (c u e)"),
            )

        def p_transpose(gb, h, dum=()):
            for g in range(KD):
                if g in dum:
                    dummy(2)
                bank = psum.tile([P, 512], F32, name="obank")
                for u in range(2):
                    for i in range(2):
                        words = p_raw[gb][h][:, i, :].bitcast(F32)
                        nc.tensor.transpose(
                            bank[:, u * 256 + i * P : u * 256 + (i + 1) * P],
                            words[:, 256 * g + u : 256 * (g + 1) : 2],
                            ident[:],
                        )
                banks["p", gb, h, g] = bank

        def p_exit(gb, h, g, eng):
            grouped = work.tile([P, 256, 4], BF16, name="p_group", align_bytes=64, bufs=8)
            dst = grouped[:].rearrange("p c t -> p (c t)").bitcast(F32).rearrange("p (c u) -> p c u", u=2)
            bank_view = banks["p", gb, h, g][:].rearrange("p (u c) -> p c u", u=2)
            if eng == "s":
                nc.scalar.copy(out=dst, in_=bank_view)
            else:
                nc.vector.tensor_copy(out=dst, in_=bank_view)
            p_group[gb, h, g] = grouped

        def p_quant(gb, h, g):
            cols = slice(gb * 512 + h * 256, gb * 512 + h * 256 + 256)
            nc.vector.quantize_mx(
                out=p_codes[g][:, cols].bitcast(FP8X4),
                scales=p_scales[g][:, cols],
                in_=p_group[gb, h, g][:].rearrange("p c t -> p (c t)"),
            )

        def project(s, gb):
            th = work.tile([P, 4, SLAB], F32, name="th")
            for tp in range(2):
                bank = psum.tile([P, 2, SLAB], F32, name="hbank", bufs=2)
                for t2 in range(2):
                    c0 = gb * 512 + (tp * 2 + t2) * P
                    for g in range(KD):
                        nc.tensor.matmul_mx(
                            out=bank[:, t2, :],
                            lhsT=p_codes[g][:, c0 : c0 + P].bitcast(FP8X4),
                            lhsT_scale=p_scales[g][:, c0 : c0 + P],
                            rhs=q_codes[s][:, g, :].bitcast(FP8X4),
                            rhs_scale=q_scales[s][:, g, :],
                            start=(g == 0),
                            stop=(g == KD - 1),
                        )
                for t2 in range(2):
                    t = tp * 2 + t2
                    nc.scalar.activation(out=th[:, t, :], in_=bank[:, t2, :], func=ACT.Tanh, bias=off[:, gb * 4 + t : gb * 4 + t + 1])
            tanh_out[s, gb] = th

        def weight(s, gb):
            zg = work.tile([P, SLAB, 4], BF16, name="z_group", align_bytes=64)
            nc.vector.tensor_tensor(
                out=zg[:].rearrange("p (c i) t -> p c t i", i=4),
                in0=tanh_out[s, gb][:].rearrange("p t (c i) -> p c t i", i=4),
                in1=gain[:, gb * 4 : gb * 4 + 4].rearrange("p (o t i) -> p o t i", o=1, i=1).to_broadcast([P, SLAB // 4, 4, 4]),
                op=MULT,
            )
            z_group[s, gb] = zg

        def z_quant(s, gb):
            nc.vector.quantize_mx(
                out=z_codes[s][:, gb, :].bitcast(FP8X4),
                scales=z_scales[s][:, gb, :],
                in_=z_group[s, gb][:].rearrange("p n t -> p (n t)"),
            )

        def score(s, i, engines):
            for half in range(2):
                ot = work.tile([P, 2, NB], F32, name="ot", bufs=8)
                for b in range(2):
                    d = half * 2 + b
                    bank = psum.tile([P, NB], F32, name="obank")
                    for gb in range(KB):
                        nc.tensor.matmul_mx(
                            out=bank[:],
                            lhsT=z_codes[s][:, gb, i * P : (i + 1) * P].bitcast(FP8X4),
                            lhsT_scale=z_scales[s][:, gb, i * P : (i + 1) * P],
                            rhs=c_codes[:, gb, d * 2 * NB : (d + 1) * 2 * NB].bitcast(FP4X4),
                            rhs_scale=c_scales[:, gb, d * NB : (d + 1) * NB],
                            start=(gb == 0),
                            stop=(gb == KB - 1),
                        )
                    if engines[d] == "s":
                        nc.scalar.copy(out=ot[:, b, :], in_=bank[:])
                    else:
                        nc.vector.tensor_copy(out=ot[:, b, :], in_=bank[:])
                    if s == NS - 1 and i == 1:
                        nc.sync.dma_start(out=out_view[s, i][:, d * NB : (d + 1) * NB], in_=ot[:, b, :])
                if not (s == NS - 1 and i == 1):
                    nc.sync.dma_start(out=out_view[s, i][:, half * 1024 : (half + 1) * 1024], in_=ot[:].rearrange("p b n -> p (b n)"))

        with tc.manual_schedule():
            load_q(0, 2)
            nc.scalar.dma_start(out=q_scale[:].rearrange("p (g t) -> p g t", t=4), in_=queries_scale.rearrange("o (g p t) -> p (o g) t", p=P, t=4))
            nc.vector.memset(zeros[:], 0.0)
            dummy(8)
            nc.vector.memset(ones[:], 1.0)
            nc.scalar.activation(out=warm[:], in_=ones[:], func=ACT.Tanh)
            make_identity(nc, ident[:])
            nc.gpsimd.memset(c_scales[:].rearrange("p g n -> p (g n)").bitcast(U32), 0)
            load_q(1)
            load_p(0, 0)
            load_p(0, 1)
            load_p(1, 0)
            load_p(1, 1)
            nc.sync.dma_start(out=off[:].rearrange("p (g t) -> p g t", t=4), in_=offset.rearrange("(g p t) -> p g t", p=P, t=4))
            nc.sync.dma_start(out=gain[:].rearrange("p (g t) -> p g t", t=4), in_=bit_gain.rearrange("(g p t) -> p g t", p=P, t=4))
            load_q(2)
            nc.sync.dma_start(out=c_codes[:].rearrange("p g n -> p g n").bitcast(I32), in_=codes_words.rearrange("g p n -> p g n").bitcast(I32))
            for qd in range(4):
                nc.sync.dma_start(
                    out=c_scales[32 * qd : 32 * qd + 4, :, :].bitcast(I32),
                    in_=codes_scales.rearrange("g q n -> q g n")[4 * qd : 4 * qd + 4].bitcast(I32),
                )
            load_q(3)

            def exits(gb, h, engs="sss"):
                for g in range(KD):
                    p_exit(gb, h, g, engs[g])

            def quants(gb, h):
                for g in range(KD):
                    p_quant(gb, h, g)

            def xq(s, a):
                for g in a:
                    q_exit(s, g)
                    if g > 0:
                        q_quant(s, g - 1)
            cast(0, parts=2)
            q_transpose(0)
            cast(1)
            p_transpose(0, 0)
            exits(0, 0)
            q_exit(0, 0)
            q_exit(0, 1)
            q_quant(0, 0)
            q_exit(0, 2)
            q_quant(0, 1)
            quants(0, 0)
            q_quant(0, 2)
            p_transpose(0, 1, (0,))
            exits(0, 1)
            quants(0, 1)
            q_transpose(1)
            p_transpose(1, 0)
            exits(1, 0)
            quants(1, 0)
            p_transpose(1, 1, (0,))
            exits(1, 1)
            project(0, 0)
            q_exit(1, 0)
            quants(1, 1)
            project(0, 1)
            q_exit(1, 1)
            q_quant(1, 0)
            q_exit(1, 2)
            q_quant(1, 1)
            q_quant(1, 2)
            project(1, 0)
            cast(2)
            weight(0, 0)
            project(1, 1)
            q_transpose(2)
            weight(0, 1)
            z_quant(0, 0)
            z_quant(0, 1)
            q_exit(2, 0)
            q_exit(2, 1)
            q_quant(2, 0)
            cast(3)
            score(0, 0, "ssss")
            q_exit(2, 2)
            q_quant(2, 1)
            q_quant(2, 2)
            weight(1, 0)
            weight(1, 1)
            z_quant(1, 0)
            score(0, 1, "ssss")
            q_transpose(3)
            project(2, 0)
            z_quant(1, 1)
            q_exit(3, 0)
            project(2, 1)
            q_exit(3, 1)
            q_quant(3, 0)
            q_exit(3, 2)
            q_quant(3, 1)
            score(1, 0, "ssss")
            q_quant(3, 2)
            weight(2, 0)
            weight(2, 1)
            z_quant(2, 0)
            score(1, 1, "ssss")
            project(3, 0)
            z_quant(2, 1)
            project(3, 1)
            weight(3, 0)
            score(2, 0, "ssss")
            weight(3, 1)
            z_quant(3, 0)
            z_quant(3, 1)
            score(2, 1, "ssvs")
            score(3, 0, "svsv")
            score(3, 1, "svsv")
